import numpy as np
import ml_dtypes


def mxq(x, axis, fmt="e4m3"):
    dtype, down = {"e4m3": (ml_dtypes.float8_e4m3fn, 7), "e5m2": (ml_dtypes.float8_e5m2, 14)}[fmt]
    v = np.moveaxis(np.asarray(x, np.float32).astype(ml_dtypes.bfloat16).astype(np.float64), axis, -1)
    blocks = v.reshape(v.shape[:-1] + (-1, 32))
    amax = np.abs(blocks).max(-1, keepdims=True)
    byte = np.maximum(np.where(amax > 0, np.frexp(amax)[1] - 1 + 127, 0) - down, 1)
    scale = np.exp2(byte - 127.0)
    codes = (blocks / scale).astype(np.float32).astype(dtype).astype(np.float64)
    return np.moveaxis((codes * scale).reshape(v.shape), -1, axis)


WIDE = False


def mx_kscale(k):
    if not WIDE:
        return np.ones(k)
    levels = np.array([30, -30])
    if k % 512:
        return np.exp2(np.random.permutation(np.resize(levels, k // 32))).repeat(32)
    a = np.empty((k // 512, 16))
    for p in range(k // 512):
        a[p, :8] = np.random.permutation(np.resize(levels, 8))
        for g in range(8):
            far = levels[np.abs(levels - a[p, g]) >= 10]
            a[p, g + 8] = far[np.random.randint(len(far))]
    return np.exp2(a.ravel()).repeat(32)


def f64(x):
    return np.asarray(x).astype(np.float64)


def striped(idx):
    return np.tile(idx.reshape(-1, 16).T, (8, 1)).astype(np.uint16)


def unstriped(offs):
    return offs[:16].T.reshape(-1).astype(np.int64)


E2M1 = np.array([0.0, 0.5, 1.0, 1.5, 2.0, 3.0, 4.0, 6.0, -0.0, -0.5, -1.0, -1.5, -2.0, -3.0, -4.0, -6.0])


def pack_weight(w, fmt):
    k, n = w.shape
    w = f64(np.asarray(w, np.float32).astype(ml_dtypes.bfloat16)).reshape(k // 32, 32, n)
    amax = np.abs(w).max(1)
    if fmt == "e4m3":
        byte = np.frexp(amax)[1] - 1 + 127 - 7
    else:
        mant, ex = np.frexp(amax / 6.0)
        byte = np.where(mant > 0.5, ex, ex - 1) + 127
    byte = np.clip(np.where(amax > 0, byte, 1), 1, 254)
    scaled = (w * np.exp2(127.0 - byte)[:, None, :]).reshape(k, n).astype(np.float32)
    by_word = np.ascontiguousarray(scaled.reshape(k // 512, 128, 4, n).transpose(0, 1, 3, 2))
    if fmt == "e4m3":
        words = by_word.astype(ml_dtypes.float8_e4m3fn).view(np.uint8)
    else:
        c = by_word.astype(ml_dtypes.float4_e2m1fn).view(np.uint8) & 0xF
        words = (c[..., 0::2] | (c[..., 1::2] << 4)).reshape(k // 512, 128, 2 * n)
    return np.ascontiguousarray(words), np.ascontiguousarray(byte.astype(np.uint8).reshape(k // 512, 16, n))


def unpack_weight(words, scales, fmt):
    g, _, n = scales.shape
    words = np.ascontiguousarray(words).reshape(g, 128, n, -1)
    if fmt == "e4m3":
        vals = words.view(ml_dtypes.float8_e4m3fn).astype(np.float64)
    else:
        nib = np.empty((g, 128, n, 4), np.uint8)
        nib[..., 0::2] = words & 0xF
        nib[..., 1::2] = words >> 4
        vals = E2M1[nib]
    vals = vals * np.repeat(np.exp2(scales.astype(np.float64) - 127.0), 8, axis=1)[..., None]
    return vals.transpose(0, 1, 3, 2).reshape(g * 512, n)


def d_silu(v):
    s = 1.0 / (1.0 + np.exp(-np.maximum(v, -700.0)))
    return s * (1.0 + v * (1.0 - s))


K, T, E, C, H, N = 768, 2048, 4, 512, 512, 512


def by_expert(wq, xq):
    return np.concatenate([wq[e].T @ xq[:, e * C:(e + 1) * C] for e in range(E)], axis=1)


def setup_inputs():
    n = np.random.standard_normal
    s = mx_kscale(N)[:, None]
    u = mx_kscale(H)
    w2 = [pack_weight(m, "e2m1") for m in n((E, N, H)) / np.sqrt(N) / s[None] * u[None, None, :]]
    w1 = [pack_weight(m, "e2m1") for m in n((E, H, K)) / np.sqrt(H) / u[None, :, None]]
    return {
        "dyT": (n((N, T)) * s).astype(np.float32),
        "a": n((H, E * C)).astype(np.float32),
        "w2_words": np.stack([m[0] for m in w2]),
        "w2_scales": np.stack([m[1] for m in w2]),
        "w1_words": np.stack([m[0] for m in w1]),
        "w1_scales": np.stack([m[1] for m in w1]),
        "gate": np.tile(np.random.uniform(0.2, 1.0, E * C), (N, 1)).astype(np.float32),
        "offs": striped(np.random.permutation(T)[:E * C]),
    }


def reference(dyT, a, w2_words, w2_scales, w1_words, w1_scales, gate, offs):
    idx = unstriped(offs)
    w2 = np.stack([unpack_weight(w2_words[e], w2_scales[e], "e2m1") for e in range(E)])
    w1 = np.stack([unpack_weight(w1_words[e], w1_scales[e], "e2m1") for e in range(E)])
    gq = mxq(f64(gate) * f64(dyT)[:, idx], 0, "e5m2")
    dh = by_expert(w2, gq)
    da = dh * d_silu(f64(a))
    dx = by_expert(w1, mxq(da, 0, "e5m2"))
    out = np.zeros((K, T))
    out[:, idx] = dx
    return out

@@ -1,0 +1,175 @@
+from contextlib import ExitStack
+
+import concourse.mybir as mybir
+
+K, T, E, C, H, N = 768, 2048, 4, 512, 512, 512
+P = 128
+PACK = 4
+K_TILES = K // P
+
+F32 = mybir.dt.float32
+BF16 = mybir.dt.bfloat16
+I32 = mybir.dt.int32
+U32 = mybir.dt.uint32
+U16 = mybir.dt.uint16
+U8 = mybir.dt.uint8
+FP4X4 = mybir.dt.float4_e2m1fn_x4
+FP8X4 = mybir.dt.float8_e5m2_x4
+ACT = mybir.ActivationFunctionType
+ALU = mybir.AluOpType
+
+FLOPS = 2 * E * C * (N * H + H * K)
+BYTES = 4 * (N * T + H * E * C + E * C + K * T) + 2 * E * C + E * (N * H + H * K) * 17 // 32
+
+
+def tile_moe_bdx_mlp_silu_kernel(tc, dyT, a, w2_words, w2_scales, w1_words, w1_scales, gate, offs, out):
+    nc = tc.nc
+    with ExitStack() as ctx:
+        keep = ctx.enter_context(tc.tile_pool(name="keep", bufs=1))
+        ring = ctx.enter_context(tc.tile_pool(name="ring", bufs=2))
+        psum_h = ctx.enter_context(tc.psum_pool(name="psum_h", bufs=4))
+        psum_x = ctx.enter_context(tc.psum_pool(name="psum_x", bufs=4))
+
+        offsets = keep.tile([P, E * C // 16], U16, name="offsets")
+        gates = keep.tile([P, E * C], F32, name="gates")
+        dy = [keep.tile([P, T], F32, name=f"dy{t}") for t in range(PACK)]
+        pre = [keep.tile([P, PACK, C], F32, name=f"pre{e}") for e in range(E)]
+        w2_raw = keep.tile([P, E, 2 * H], U8, name="w2_raw", align_bytes=64)
+        w2 = keep.tile([P, E, 2 * H], U8, name="w2", align_bytes=64)
+        w2_sraw = keep.tile([P, E, H], U8, name="w2_sraw", align_bytes=64)
+        w2_s = keep.tile([P, E, H], U8, name="w2_s", align_bytes=64)
+        w1 = keep.tile([P, E, 2 * K], U8, name="w1", align_bytes=64)
+        w1_s = keep.tile([P, E, K], U8, name="w1_s", align_bytes=64)
+        window = [keep.tile([P, T], F32, name=f"window{m}") for m in range(K_TILES)]
+
+        nc.vector.memset(w2_sraw[:].bitcast(I32), 0)
+        nc.vector.memset(w1_s[:].bitcast(I32), 0)
+
+        dy_rows = dyT.rearrange("(p t) j -> p t j", t=PACK)
+        a_rows = a.rearrange("(p t) j -> p t j", t=PACK)
+
+        nc.sync.dma_start(out=offsets[:], in_=offs)
+        for q in range(4):
+            nc.scalar.dma_start(
+                out=w2_sraw[32 * q : 32 * q + 4].bitcast(I32),
+                in_=w2_scales[:, 0, 4 * q : 4 * q + 4, :].rearrange("e f n -> f e n").bitcast(I32),
+            )
+        nc.sync.dma_start(out=w2_raw[:].bitcast(I32), in_=w2_words.rearrange("e o p n -> p (e o) n").bitcast(I32))
+        for t in range(PACK):
+            nc.sync.dma_start(out=gates[:, t * C : (t + 1) * C], in_=gate[0:P, t * C : (t + 1) * C])
+            nc.sync.dma_start(out=dy[t][:], in_=dy_rows[:, t, :])
+        nc.sync.dma_start(out=pre[0][:], in_=a_rows[:, :, 0:C])
+        for q in range(4):
+            nc.scalar.dma_start(
+                out=w1_s[32 * q : 32 * q + 4].bitcast(I32),
+                in_=w1_scales[:, 0, 4 * q : 4 * q + 4, :].rearrange("e f n -> f e n").bitcast(I32),
+            )
+        nc.sync.dma_start(out=w1[:].bitcast(I32), in_=w1_words.rearrange("e o p n -> p (e o) n").bitcast(I32))
+        for e in range(1, E):
+            nc.sync.dma_start(out=pre[e][:], in_=a_rows[:, :, e * C : (e + 1) * C])
+
+        nc.vector.tensor_copy(
+            out=w2[:].bitcast(U16).rearrange("p e (t m) -> p e m t", t=PACK),
+            in_=w2_raw[:].bitcast(U16).rearrange("p e (m t) -> p e m t", t=PACK),
+        )
+        nc.vector.tensor_copy(
+            out=w2_s[:].rearrange("p e (t m) -> p e m t", t=PACK),
+            in_=w2_sraw[:].rearrange("p e (m t) -> p e m t", t=PACK),
+        )
+
+        def slots(e):
+            return offsets[:, e * C // 16 : (e + 1) * C // 16]
+
+        def derivative(e):
+            other = ring.tile([P, PACK, C], F32, name="other")
+            if e % 2 == 0:
+                nc.scalar.activation(other[:], pre[e][:], ACT.Sigmoid)
+                nc.scalar.activation(pre[e][:], pre[e][:], ACT.Silu, scale=-1.0)
+                z, s = pre[e], other
+            else:
+                nc.scalar.activation(other[:], pre[e][:], ACT.Silu, scale=-1.0)
+                nc.scalar.activation(pre[e][:], pre[e][:], ACT.Sigmoid)
+                z, s = other, pre[e]
+            if e == 0:
+                nc.vector.scalar_tensor_tensor(out=other[:], in0=z[:], scalar=1.0, in1=s[:], op0=ALU.subtract, op1=ALU.mult)
+            else:
+                nc.scalar.activation(z[:], z[:], ACT.Identity, bias=1.0, scale=-1.0)
+                nc.gpsimd.tensor_tensor(other[:], z[:], s[:], ALU.mult)
+            return other
+
+        def quantize(grouped, kind, depth):
+            codes = ring.tile([P, C], U32, name=f"codes_{kind}", align_bytes=64, bufs=depth)
+            scales = ring.tile([P, C], U8, name=f"scales_{kind}", align_bytes=64, bufs=depth)
+            nc.vector.quantize_mx(out=codes[:].bitcast(FP8X4), scales=scales[:], in_=grouped[:].rearrange("p c t -> p (c t)"))
+            return codes, scales
+
+        def gather(e):
+            g = ring.tile([P, PACK, C], F32, name="g")
+            for t in range(PACK):
+                nc.vector.tensor_tensor(g[:, t, :], dy[t][:].indirect(slots(e)), gates[:, e * C : (e + 1) * C], ALU.mult)
+            g_grouped = ring.tile([P, C, PACK], BF16, name="g_grouped", align_bytes=64)
+            nc.scalar.copy(out=g_grouped[:], in_=g[:].rearrange("p t c -> p c t"))
+            return quantize(g_grouped, "g", E)
+
+        def multiply(e, g_codes, g_scales):
+            minus_d = derivative(e)
+            if e == 0:
+                da = ring.tile([P, PACK, C], BF16, name="da", align_bytes=64, bufs=1)
+            else:
+                da = ring.tile([P, PACK, C], F32, name="dh_copy", align_bytes=64, bufs=1)
+            for t in range(PACK):
+                dh = psum_h.tile([P, C], F32, name="dh")
+                nc.tensor.matmul_mx(
+                    out=dh[:],
+                    lhsT=w2[:, e, 2 * P * t : 2 * P * (t + 1)].bitcast(FP4X4),
+                    lhsT_scale=w2_s[:, e, P * t : P * (t + 1)],
+                    rhs=g_codes[:].bitcast(FP8X4),
+                    rhs_scale=g_scales[:],
+                    start=True,
+                    stop=True,
+                )
+                if e == 0:
+                    nc.vector.scalar_tensor_tensor(
+                        out=da[:, t, :], in0=dh[:], scalar=-1.0, in1=minus_d[:, t, :], op0=ALU.mult, op1=ALU.mult
+                    )
+                else:
+                    nc.scalar.copy(out=da[:, t, :], in_=dh[:])
+            da_grouped = ring.tile([P, C, PACK], BF16, name="da_grouped", align_bytes=64)
+            if e == 0:
+                nc.scalar.copy(out=da_grouped[:], in_=da[:].rearrange("p t c -> p c t"))
+            else:
+                nc.gpsimd.tensor_tensor(
+                    da_grouped[:], da[:].rearrange("p t c -> p c t"), minus_d[:].rearrange("p t c -> p c t"), ALU.mult
+                )
+            da_codes, da_scales = quantize(da_grouped, "da", 2)
+            results = []
+            for m in range(K_TILES):
+                dx = psum_x.tile([P, C], F32, name="dx")
+                nc.tensor.matmul_mx(
+                    out=dx[:],
+                    lhsT=w1[:, e, 2 * P * m : 2 * P * (m + 1)].bitcast(FP4X4),
+                    lhsT_scale=w1_s[:, e, P * m : P * (m + 1)],
+                    rhs=da_codes[:].bitcast(FP8X4),
+                    rhs_scale=da_scales[:],
+                    start=True,
+                    stop=True,
+                )
+                result = ring.tile([P, C], F32, name="result", bufs=8)
+                nc.scalar.copy(out=result[:], in_=dx[:])
+                results.append(result)
+            return results
+
+        def put_back(e, results):
+            for m in range(K_TILES):
+                nc.vector.tensor_copy(window[m][:].indirect(slots(e)), results[m][:])
+                if e == E - 1:
+                    nc.sync.dma_start(out=out[m * P : (m + 1) * P, :], in_=window[m][:])
+
+        codes = [gather(0)]
+        ready = multiply(0, *codes[0])
+        codes += [gather(e) for e in range(1, E)]
+        for e in range(1, E):
+            following = multiply(e, *codes[e])
+            put_back(e - 1, ready)
+            ready = following
+        put_back(E - 1, ready)

@@ -44,28 +44,34 @@ def tile_moe_bdx_mlp_silu_kernel(tc, dyT, a, w2_words, w2_scales, w1_words, w1_s
 
         nc.vector.memset(w2_sraw[:].bitcast(I32), 0)
         nc.vector.memset(w1_s[:].bitcast(I32), 0)
+        warm = keep.tile([P, 8], F32, name="warm")
+        nc.vector.memset(warm[:], 0.0)
+        nc.scalar.activation(warm[:], warm[:], ACT.Sigmoid)
 
         dy_rows = dyT.rearrange("(p t) j -> p t j", t=PACK)
         a_rows = a.rearrange("(p t) j -> p t j", t=PACK)
 
+        def load_scales(planes, scales):
+            for q in range(4):
+                nc.sync.dma_start(
+                    out=planes[32 * q : 32 * q + 4].bitcast(I32),
+                    in_=scales[:, 0, 4 * q : 4 * q + 4, :].rearrange("e f n -> f e n").bitcast(I32),
+                )
+
         nc.sync.dma_start(out=offsets[:], in_=offs)
-        for q in range(4):
-            nc.scalar.dma_start(
-                out=w2_sraw[32 * q : 32 * q + 4].bitcast(I32),
-                in_=w2_scales[:, 0, 4 * q : 4 * q + 4, :].rearrange("e f n -> f e n").bitcast(I32),
-            )
+        load_scales(w2_sraw, w2_scales)
         nc.sync.dma_start(out=w2_raw[:].bitcast(I32), in_=w2_words.rearrange("e o p n -> p (e o) n").bitcast(I32))
-        for t in range(PACK):
-            nc.sync.dma_start(out=gates[:, t * C : (t + 1) * C], in_=gate[0:P, t * C : (t + 1) * C])
-            nc.sync.dma_start(out=dy[t][:], in_=dy_rows[:, t, :])
+        nc.sync.dma_start(out=gates[:, 0:C], in_=gate[0:P, 0:C])
+        nc.sync.dma_start(out=dy[0][:], in_=dy_rows[:, 0, :])
+        nc.sync.dma_start(out=gates[:, C:], in_=gate[0:P, C:])
+        nc.sync.dma_start(out=dy[1][:], in_=dy_rows[:, 1, :])
         nc.sync.dma_start(out=pre[0][:], in_=a_rows[:, :, 0:C])
-        for q in range(4):
-            nc.scalar.dma_start(
-                out=w1_s[32 * q : 32 * q + 4].bitcast(I32),
-                in_=w1_scales[:, 0, 4 * q : 4 * q + 4, :].rearrange("e f n -> f e n").bitcast(I32),
-            )
+        nc.sync.dma_start(out=dy[2][:], in_=dy_rows[:, 2, :])
+        nc.sync.dma_start(out=dy[3][:], in_=dy_rows[:, 3, :])
+        nc.sync.dma_start(out=pre[1][:], in_=a_rows[:, :, C : 2 * C])
+        load_scales(w1_s, w1_scales)
         nc.sync.dma_start(out=w1[:].bitcast(I32), in_=w1_words.rearrange("e o p n -> p (e o) n").bitcast(I32))
-        for e in range(1, E):
+        for e in range(2, E):
             nc.sync.dma_start(out=pre[e][:], in_=a_rows[:, :, e * C : (e + 1) * C])
 
         nc.vector.tensor_copy(
@@ -104,19 +110,18 @@ def tile_moe_bdx_mlp_silu_kernel(tc, dyT, a, w2_words, w2_scales, w1_words, w1_s
             return codes, scales
 
         def gather(e):
-            g = ring.tile([P, PACK, C], F32, name="g")
+            g = ring.tile([P, PACK, C], F32, name="g", bufs=3)
             for t in range(PACK):
                 nc.vector.tensor_tensor(g[:, t, :], dy[t][:].indirect(slots(e)), gates[:, e * C : (e + 1) * C], ALU.mult)
             g_grouped = ring.tile([P, C, PACK], BF16, name="g_grouped", align_bytes=64)
             nc.scalar.copy(out=g_grouped[:], in_=g[:].rearrange("p t c -> p c t"))
             return quantize(g_grouped, "g", E)
 
-        def multiply(e, g_codes, g_scales):
-            minus_d = derivative(e)
+        def multiply(e, minus_d, g_codes, g_scales):
             if e == 0:
                 da = ring.tile([P, PACK, C], BF16, name="da", align_bytes=64, bufs=1)
             else:
-                da = ring.tile([P, PACK, C], F32, name="dh_copy", align_bytes=64, bufs=1)
+                da = ring.tile([P, PACK, C], F32, name="dh_copy", bufs=1)
             for t in range(PACK):
                 dh = psum_h.tile([P, C], F32, name="dh")
                 nc.tensor.matmul_mx(
@@ -134,7 +139,7 @@ def tile_moe_bdx_mlp_silu_kernel(tc, dyT, a, w2_words, w2_scales, w1_words, w1_s
                     )
                 else:
                     nc.scalar.copy(out=da[:, t, :], in_=dh[:])
-            da_grouped = ring.tile([P, C, PACK], BF16, name="da_grouped", align_bytes=64)
+            da_grouped = ring.tile([P, C, PACK], BF16, name="da_grouped", align_bytes=64, bufs=1)
             if e == 0:
                 nc.scalar.copy(out=da_grouped[:], in_=da[:].rearrange("p t c -> p c t"))
             else:
@@ -142,34 +147,51 @@ def tile_moe_bdx_mlp_silu_kernel(tc, dyT, a, w2_words, w2_scales, w1_words, w1_s
                     da_grouped[:], da[:].rearrange("p t c -> p c t"), minus_d[:].rearrange("p t c -> p c t"), ALU.mult
                 )
             da_codes, da_scales = quantize(da_grouped, "da", 2)
+            return da_codes, da_scales
+
+        def project(e, m, da_codes, da_scales, result):
+            dx = psum_x.tile([P, C], F32, name="dx")
+            nc.tensor.matmul_mx(
+                out=dx[:],
+                lhsT=w1[:, e, 2 * P * m : 2 * P * (m + 1)].bitcast(FP4X4),
+                lhsT_scale=w1_s[:, e, P * m : P * (m + 1)],
+                rhs=da_codes[:].bitcast(FP8X4),
+                rhs_scale=da_scales[:],
+                start=True,
+                stop=True,
+            )
+            nc.scalar.copy(out=result, in_=dx[:])
+
+        def project_first(e, operand):
             results = []
-            for m in range(K_TILES):
-                dx = psum_x.tile([P, C], F32, name="dx")
-                nc.tensor.matmul_mx(
-                    out=dx[:],
-                    lhsT=w1[:, e, 2 * P * m : 2 * P * (m + 1)].bitcast(FP4X4),
-                    lhsT_scale=w1_s[:, e, P * m : P * (m + 1)],
-                    rhs=da_codes[:].bitcast(FP8X4),
-                    rhs_scale=da_scales[:],
-                    start=True,
-                    stop=True,
-                )
-                result = ring.tile([P, C], F32, name="result", bufs=8)
-                nc.scalar.copy(out=result[:], in_=dx[:])
-                results.append(result)
+            for m in range(K_TILES - 2):
+                result = ring.tile([P, C], F32, name="result", bufs=6)
+                project(e, m, *operand, result[:])
+                results.append(result[:])
             return results
+
+        def project_last(e, operand):
+            pair = ring.tile([P, 2, C], F32, name="pair", tag="da_grouped", align_bytes=64, bufs=1)
+            for i in range(2):
+                project(e, K_TILES - 2 + i, *operand, pair[:, i, :])
+            return [pair[:, 0, :], pair[:, 1, :]]
 
         def put_back(e, results):
             for m in range(K_TILES):
-                nc.vector.tensor_copy(window[m][:].indirect(slots(e)), results[m][:])
+                nc.vector.tensor_copy(window[m][:].indirect(slots(e)), results[m])
                 if e == E - 1:
                     nc.sync.dma_start(out=out[m * P : (m + 1) * P, :], in_=window[m][:])
 
         codes = [gather(0)]
-        ready = multiply(0, *codes[0])
+        operand = multiply(0, derivative(0), *codes[0])
+        first = project_first(0, operand)
+        minus_d = derivative(1)
         codes += [gather(e) for e in range(1, E)]
         for e in range(1, E):
-            following = multiply(e, *codes[e])
-            put_back(e - 1, ready)
-            ready = following
-        put_back(E - 1, ready)
+            following = multiply(e, minus_d, *codes[e])
+            put_back(e - 1, first + project_last(e - 1, operand))
+            operand = following
+            first = project_first(e, operand)
+            if e + 1 < E:
+                minus_d = derivative(e + 1)
+        put_back(E - 1, first + project_last(E - 1, operand))

@@ -32,7 +32,7 @@ def tile_moe_bdx_mlp_silu_kernel(tc, dyT, a, w2_words, w2_scales, w1_words, w1_s
 
         offsets = keep.tile([P, E * C // 16], U16, name="offsets")
         gates = keep.tile([P, E * C], F32, name="gates")
-        dy = [keep.tile([P, T], F32, name=f"dy{t}") for t in range(PACK)]
+        dy = [keep.tile([P, T], F32, name=f"dy{t}", tag=f"columns{t}") for t in range(PACK)]
         pre = [keep.tile([P, PACK, C], F32, name=f"pre{e}") for e in range(E)]
         w2_raw = keep.tile([P, E, 2 * H], U8, name="w2_raw", align_bytes=64)
         w2 = keep.tile([P, E, 2 * H], U8, name="w2", align_bytes=64)
@@ -40,7 +40,6 @@ def tile_moe_bdx_mlp_silu_kernel(tc, dyT, a, w2_words, w2_scales, w1_words, w1_s
         w2_s = keep.tile([P, E, H], U8, name="w2_s", align_bytes=64)
         w1 = keep.tile([P, E, 2 * K], U8, name="w1", align_bytes=64)
         w1_s = keep.tile([P, E, K], U8, name="w1_s", align_bytes=64)
-        window = [keep.tile([P, T], F32, name=f"window{m}") for m in range(K_TILES)]
 
         nc.vector.memset(w2_sraw[:].bitcast(I32), 0)
         nc.vector.memset(w1_s[:].bitcast(I32), 0)
@@ -60,7 +59,10 @@ def tile_moe_bdx_mlp_silu_kernel(tc, dyT, a, w2_words, w2_scales, w1_words, w1_s
 
         nc.sync.dma_start(out=offsets[:], in_=offs)
         load_scales(w2_sraw, w2_scales)
-        nc.sync.dma_start(out=w2_raw[:].bitcast(I32), in_=w2_words.rearrange("e o p n -> p (e o) n").bitcast(I32))
+        for e in (0, 2):
+            nc.sync.dma_start(
+                out=w2_raw[:, e : e + 2].bitcast(I32), in_=w2_words[e : e + 2].rearrange("e o p n -> p (e o) n").bitcast(I32)
+            )
         nc.sync.dma_start(out=gates[:, 0:C], in_=gate[0:P, 0:C])
         nc.sync.dma_start(out=dy[0][:], in_=dy_rows[:, 0, :])
         nc.sync.dma_start(out=gates[:, C:], in_=gate[0:P, C:])
@@ -75,13 +77,14 @@ def tile_moe_bdx_mlp_silu_kernel(tc, dyT, a, w2_words, w2_scales, w1_words, w1_s
             nc.sync.dma_start(out=pre[e][:], in_=a_rows[:, :, e * C : (e + 1) * C])
 
         nc.vector.tensor_copy(
-            out=w2[:].bitcast(U16).rearrange("p e (t m) -> p e m t", t=PACK),
-            in_=w2_raw[:].bitcast(U16).rearrange("p e (m t) -> p e m t", t=PACK),
-        )
-        nc.vector.tensor_copy(
             out=w2_s[:].rearrange("p e (t m) -> p e m t", t=PACK),
             in_=w2_sraw[:].rearrange("p e (m t) -> p e m t", t=PACK),
         )
+        for e in (0, 2):
+            nc.vector.tensor_copy(
+                out=w2[:, e : e + 2].bitcast(U16).rearrange("p e (t m) -> p e m t", t=PACK),
+                in_=w2_raw[:, e : e + 2].bitcast(U16).rearrange("p e (m t) -> p e m t", t=PACK),
+            )
 
         def slots(e):
             return offsets[:, e * C // 16 : (e + 1) * C // 16]
@@ -96,12 +99,22 @@ def tile_moe_bdx_mlp_silu_kernel(tc, dyT, a, w2_words, w2_scales, w1_words, w1_s
                 nc.scalar.activation(other[:], pre[e][:], ACT.Silu, scale=-1.0)
                 nc.scalar.activation(pre[e][:], pre[e][:], ACT.Sigmoid)
                 z, s = other, pre[e]
-            if e == 0:
+            if e < 2:
                 nc.vector.scalar_tensor_tensor(out=other[:], in0=z[:], scalar=1.0, in1=s[:], op0=ALU.subtract, op1=ALU.mult)
-            else:
-                nc.scalar.activation(z[:], z[:], ACT.Identity, bias=1.0, scale=-1.0)
-                nc.gpsimd.tensor_tensor(other[:], z[:], s[:], ALU.mult)
-            return other
+                return other[:]
+            nc.scalar.activation(z[:], z[:], ACT.Identity, bias=-1.0)
+            return z, s
+
+        def in_turn(i, shape, dtype, name):
+            return ring.tile(shape, dtype, name=name, tag=f"turn{i % 2}", align_bytes=64, bufs=1)
+
+        def staging(e):
+            return in_turn(e, [P, PACK + 2, C], F32, "staging")
+
+        def product(stage, z, s):
+            d = stage[:, 0:PACK, :]
+            nc.gpsimd.tensor_tensor(d, z[:], s[:], ALU.mult)
+            return d
 
         def quantize(grouped, kind, depth):
             codes = ring.tile([P, C], U32, name=f"codes_{kind}", align_bytes=64, bufs=depth)
@@ -138,13 +151,13 @@ def tile_moe_bdx_mlp_silu_kernel(tc, dyT, a, w2_words, w2_scales, w1_words, w1_s
                         out=da[:, t, :], in0=dh[:], scalar=-1.0, in1=minus_d[:, t, :], op0=ALU.mult, op1=ALU.mult
                     )
                 else:
-                    nc.scalar.copy(out=da[:, t, :], in_=dh[:])
-            da_grouped = ring.tile([P, C, PACK], BF16, name="da_grouped", align_bytes=64, bufs=1)
+                    nc.scalar.activation(da[:, t, :], dh[:], ACT.Copy, scale=-1.0)
+            da_grouped = in_turn(max(e, 1), [P, C, PACK], BF16, "da_grouped")
             if e == 0:
                 nc.scalar.copy(out=da_grouped[:], in_=da[:].rearrange("p t c -> p c t"))
             else:
                 nc.gpsimd.tensor_tensor(
-                    da_grouped[:], da[:].rearrange("p t c -> p c t"), minus_d[:].rearrange("p t c -> p c t"), ALU.mult
+                    da_grouped[:], da[:].rearrange("p t c -> p c t"), minus_d.rearrange("p t c -> p c t"), ALU.mult
                 )
             da_codes, da_scales = quantize(da_grouped, "da", 2)
             return da_codes, da_scales
@@ -170,11 +183,10 @@ def tile_moe_bdx_mlp_silu_kernel(tc, dyT, a, w2_words, w2_scales, w1_words, w1_s
                 results.append(result[:])
             return results
 
-        def project_last(e, operand):
-            pair = ring.tile([P, 2, C], F32, name="pair", tag="da_grouped", align_bytes=64, bufs=1)
+        def project_last(e, operand, stage):
             for i in range(2):
-                project(e, K_TILES - 2 + i, *operand, pair[:, i, :])
-            return [pair[:, 0, :], pair[:, 1, :]]
+                project(e, K_TILES - 2 + i, *operand, stage[:, PACK + i, :])
+            return [stage[:, PACK, :], stage[:, PACK + 1, :]]
 
         def put_back(e, results):
             for m in range(K_TILES):
@@ -185,13 +197,17 @@ def tile_moe_bdx_mlp_silu_kernel(tc, dyT, a, w2_words, w2_scales, w1_words, w1_s
         codes = [gather(0)]
         operand = multiply(0, derivative(0), *codes[0])
         first = project_first(0, operand)
-        minus_d = derivative(1)
+        d = derivative(1)
         codes += [gather(e) for e in range(1, E)]
+        window = [keep.tile([P, T], F32, name=f"window{m}", tag=f"columns{m}") for m in range(K_TILES)]
         for e in range(1, E):
-            following = multiply(e, minus_d, *codes[e])
-            put_back(e - 1, first + project_last(e - 1, operand))
+            following = multiply(e, d, *codes[e])
+            stage = staging(e)
+            results = first + project_last(e - 1, operand, stage)
+            if e + 1 < E:
+                d = product(stage, *derivative(e + 1))
+            put_back(e - 1, results)
             operand = following
             first = project_first(e, operand)
-            if e + 1 < E:
-                minus_d = derivative(e + 1)
-        put_back(E - 1, first + project_last(E - 1, operand))
+        stage = staging(E)
+        put_back(E - 1, first + project_last(E - 1, operand, stage))

@@ -31,7 +31,7 @@ def tile_moe_bdx_mlp_silu_kernel(tc, dyT, a, w2_words, w2_scales, w1_words, w1_s
         psum_x = ctx.enter_context(tc.psum_pool(name="psum_x", bufs=4))
 
         offsets = keep.tile([P, E * C // 16], U16, name="offsets")
-        gates = keep.tile([P, E * C], F32, name="gates")
+        gates = [keep.tile([P, C], F32, name=f"gates{e}") for e in range(E)]
         dy = [keep.tile([P, T], F32, name=f"dy{t}", tag=f"columns{t}") for t in range(PACK)]
         pre = [keep.tile([P, PACK, C], F32, name=f"pre{e}") for e in range(E)]
         w2_raw = keep.tile([P, E, 2 * H], U8, name="w2_raw", align_bytes=64)
@@ -57,33 +57,44 @@ def tile_moe_bdx_mlp_silu_kernel(tc, dyT, a, w2_words, w2_scales, w1_words, w1_s
                     in_=scales[:, 0, 4 * q : 4 * q + 4, :].rearrange("e f n -> f e n").bitcast(I32),
                 )
 
-        nc.sync.dma_start(out=offsets[:], in_=offs)
-        load_scales(w2_sraw, w2_scales)
-        for e in (0, 2):
+        def load_w2(e):
             nc.sync.dma_start(
                 out=w2_raw[:, e : e + 2].bitcast(I32), in_=w2_words[e : e + 2].rearrange("e o p n -> p (e o) n").bitcast(I32)
             )
-        nc.sync.dma_start(out=gates[:, 0:C], in_=gate[0:P, 0:C])
-        nc.sync.dma_start(out=dy[0][:], in_=dy_rows[:, 0, :])
-        nc.sync.dma_start(out=gates[:, C:], in_=gate[0:P, C:])
-        nc.sync.dma_start(out=dy[1][:], in_=dy_rows[:, 1, :])
-        nc.sync.dma_start(out=pre[0][:], in_=a_rows[:, :, 0:C])
-        nc.sync.dma_start(out=dy[2][:], in_=dy_rows[:, 2, :])
-        nc.sync.dma_start(out=dy[3][:], in_=dy_rows[:, 3, :])
-        nc.sync.dma_start(out=pre[1][:], in_=a_rows[:, :, C : 2 * C])
-        load_scales(w1_s, w1_scales)
-        nc.sync.dma_start(out=w1[:].bitcast(I32), in_=w1_words.rearrange("e o p n -> p (e o) n").bitcast(I32))
-        for e in range(2, E):
+
+        def load_gates(e):
+            nc.sync.dma_start(out=gates[e][:], in_=gate[0:P, e * C : (e + 1) * C])
+
+        def load_dy(t):
+            nc.sync.dma_start(out=dy[t][:], in_=dy_rows[:, t, :])
+
+        def load_pre(e):
             nc.sync.dma_start(out=pre[e][:], in_=a_rows[:, :, e * C : (e + 1) * C])
 
+        nc.sync.dma_start(out=offsets[:], in_=offs)
+        load_scales(w2_sraw, w2_scales)
+        load_w2(0)
+        for i in range(3):
+            load_gates(i)
+            load_dy(i)
+        load_pre(0)
+        load_dy(3)
+        load_w2(2)
+        load_gates(3)
+        load_pre(1)
+        load_scales(w1_s, w1_scales)
+        nc.sync.dma_start(out=w1[:].bitcast(I32), in_=w1_words.rearrange("e o p n -> p (e o) n").bitcast(I32))
+        load_pre(2)
+        load_pre(3)
+
         nc.vector.tensor_copy(
-            out=w2_s[:].rearrange("p e (t m) -> p e m t", t=PACK),
-            in_=w2_sraw[:].rearrange("p e (m t) -> p e m t", t=PACK),
+            out=w2_s[:].rearrange("p e (t m) -> p e t m", t=PACK),
+            in_=w2_sraw[:].rearrange("p e (m t) -> p e t m", t=PACK),
         )
         for e in (0, 2):
             nc.vector.tensor_copy(
-                out=w2[:, e : e + 2].bitcast(U16).rearrange("p e (t m) -> p e m t", t=PACK),
-                in_=w2_raw[:, e : e + 2].bitcast(U16).rearrange("p e (m t) -> p e m t", t=PACK),
+                out=w2[:, e : e + 2].bitcast(U16).rearrange("p e (t m) -> p e t m", t=PACK),
+                in_=w2_raw[:, e : e + 2].bitcast(U16).rearrange("p e (m t) -> p e t m", t=PACK),
             )
 
         def slots(e):
@@ -109,7 +120,7 @@ def tile_moe_bdx_mlp_silu_kernel(tc, dyT, a, w2_words, w2_scales, w1_words, w1_s
             return ring.tile(shape, dtype, name=name, tag=f"turn{i % 2}", align_bytes=64, bufs=1)
 
         def staging(e):
-            return in_turn(e, [P, PACK + 2, C], F32, "staging")
+            return in_turn(e, [P, PACK + 1, C], F32, "staging")
 
         def product(stage, z, s):
             d = stage[:, 0:PACK, :]
@@ -125,16 +136,15 @@ def tile_moe_bdx_mlp_silu_kernel(tc, dyT, a, w2_words, w2_scales, w1_words, w1_s
         def gather(e):
             g = ring.tile([P, PACK, C], F32, name="g", bufs=3)
             for t in range(PACK):
-                nc.vector.tensor_tensor(g[:, t, :], dy[t][:].indirect(slots(e)), gates[:, e * C : (e + 1) * C], ALU.mult)
+                nc.vector.tensor_tensor(g[:, t, :], dy[t][:].indirect(slots(e)), gates[e][:], ALU.mult)
             g_grouped = ring.tile([P, C, PACK], BF16, name="g_grouped", align_bytes=64)
             nc.scalar.copy(out=g_grouped[:], in_=g[:].rearrange("p t c -> p c t"))
             return quantize(g_grouped, "g", E)
 
         def multiply(e, minus_d, g_codes, g_scales):
-            if e == 0:
-                da = ring.tile([P, PACK, C], BF16, name="da", align_bytes=64, bufs=1)
-            else:
-                da = ring.tile([P, PACK, C], F32, name="dh_copy", bufs=1)
+            da = ring.tile([P, PACK, C], BF16, name="da", align_bytes=64, bufs=1)
+            if e > 0:
+                dh_copy = ring.tile([P, PACK, C], F32, name="dh_copy", bufs=1)
             for t in range(PACK):
                 dh = psum_h.tile([P, C], F32, name="dh")
                 nc.tensor.matmul_mx(
@@ -151,14 +161,12 @@ def tile_moe_bdx_mlp_silu_kernel(tc, dyT, a, w2_words, w2_scales, w1_words, w1_s
                         out=da[:, t, :], in0=dh[:], scalar=-1.0, in1=minus_d[:, t, :], op0=ALU.mult, op1=ALU.mult
                     )
                 else:
-                    nc.scalar.activation(da[:, t, :], dh[:], ACT.Copy, scale=-1.0)
+                    nc.scalar.activation(dh_copy[:, t, :], dh[:], ACT.Copy, scale=-1.0)
+            if e > 0:
+                for t in range(0, PACK, 2):
+                    nc.gpsimd.tensor_tensor(da[:, t : t + 2, :], dh_copy[:, t : t + 2, :], minus_d[:, t : t + 2, :], ALU.mult)
             da_grouped = in_turn(max(e, 1), [P, C, PACK], BF16, "da_grouped")
-            if e == 0:
-                nc.scalar.copy(out=da_grouped[:], in_=da[:].rearrange("p t c -> p c t"))
-            else:
-                nc.gpsimd.tensor_tensor(
-                    da_grouped[:], da[:].rearrange("p t c -> p c t"), minus_d.rearrange("p t c -> p c t"), ALU.mult
-                )
+            nc.scalar.copy(out=da_grouped[:], in_=da[:].rearrange("p t c -> p c t"))
             da_codes, da_scales = quantize(da_grouped, "da", 2)
             return da_codes, da_scales
 
@@ -177,16 +185,15 @@ def tile_moe_bdx_mlp_silu_kernel(tc, dyT, a, w2_words, w2_scales, w1_words, w1_s
 
         def project_first(e, operand):
             results = []
-            for m in range(K_TILES - 2):
+            for m in range(K_TILES - 1):
                 result = ring.tile([P, C], F32, name="result", bufs=6)
                 project(e, m, *operand, result[:])
                 results.append(result[:])
             return results
 
         def project_last(e, operand, stage):
-            for i in range(2):
-                project(e, K_TILES - 2 + i, *operand, stage[:, PACK + i, :])
-            return [stage[:, PACK, :], stage[:, PACK + 1, :]]
+            project(e, K_TILES - 1, *operand, stage[:, PACK, :])
+            return [stage[:, PACK, :]]
 
         def put_back(e, results):
             for m in range(K_TILES):

@@ -31,7 +31,6 @@ def tile_moe_bdx_mlp_silu_kernel(tc, dyT, a, w2_words, w2_scales, w1_words, w1_s
         psum_x = ctx.enter_context(tc.psum_pool(name="psum_x", bufs=4))
 
         offsets = keep.tile([P, E * C // 16], U16, name="offsets")
-        gates = [keep.tile([P, C], F32, name=f"gates{e}") for e in range(E)]
         dy = [keep.tile([P, T], F32, name=f"dy{t}", tag=f"columns{t}") for t in range(PACK)]
         pre = [keep.tile([P, PACK, C], F32, name=f"pre{e}") for e in range(E)]
         w2_raw = keep.tile([P, E, 2 * H], U8, name="w2_raw", align_bytes=64)
@@ -40,6 +39,12 @@ def tile_moe_bdx_mlp_silu_kernel(tc, dyT, a, w2_words, w2_scales, w1_words, w1_s
         w2_s = keep.tile([P, E, H], U8, name="w2_s", align_bytes=64)
         w1 = keep.tile([P, E, 2 * K], U8, name="w1", align_bytes=64)
         w1_s = keep.tile([P, E, K], U8, name="w1_s", align_bytes=64)
+
+        def in_turn(i, shape, dtype, name):
+            return ring.tile(shape, dtype, name=name, tag=f"turn{i % 2}", align_bytes=64, bufs=1)
+
+        gates = [keep.tile([P, C], F32, name=f"gates{e}") for e in range(E - 1)]
+        gates.append(in_turn(0, [P, C], F32, "gates_last"))
 
         nc.vector.memset(w2_sraw[:].bitcast(I32), 0)
         nc.vector.memset(w1_s[:].bitcast(I32), 0)
@@ -97,34 +102,40 @@ def tile_moe_bdx_mlp_silu_kernel(tc, dyT, a, w2_words, w2_scales, w1_words, w1_s
                 in_=w2_raw[:, e : e + 2].bitcast(U16).rearrange("p e (m t) -> p e t m", t=PACK),
             )
 
+        def interleave(grouped, planes):
+            nc.scalar.copy(
+                out=grouped[:].rearrange("p (c i) t -> p c t i", i=4),
+                in_=planes[:].rearrange("p t (c i) -> p c t i", i=4),
+            )
+
         def slots(e):
             return offsets[:, e * C // 16 : (e + 1) * C // 16]
 
         def derivative(e):
             other = ring.tile([P, PACK, C], F32, name="other")
             if e % 2 == 0:
-                nc.scalar.activation(other[:], pre[e][:], ACT.Sigmoid)
-                nc.scalar.activation(pre[e][:], pre[e][:], ACT.Silu, scale=-1.0)
+                for t in range(0, PACK, 2):
+                    nc.scalar.activation(other[:, t : t + 2, :], pre[e][:, t : t + 2, :], ACT.Sigmoid)
+                for t in range(0, PACK, 2):
+                    nc.scalar.activation(pre[e][:, t : t + 2, :], pre[e][:, t : t + 2, :], ACT.Silu, scale=-1.0)
                 z, s = pre[e], other
             else:
                 nc.scalar.activation(other[:], pre[e][:], ACT.Silu, scale=-1.0)
                 nc.scalar.activation(pre[e][:], pre[e][:], ACT.Sigmoid)
                 z, s = other, pre[e]
-            if e < 2:
+            if e == 0:
                 nc.vector.scalar_tensor_tensor(out=other[:], in0=z[:], scalar=1.0, in1=s[:], op0=ALU.subtract, op1=ALU.mult)
                 return other[:]
             nc.scalar.activation(z[:], z[:], ACT.Identity, bias=-1.0)
             return z, s
-
-        def in_turn(i, shape, dtype, name):
-            return ring.tile(shape, dtype, name=name, tag=f"turn{i % 2}", align_bytes=64, bufs=1)
 
         def staging(e):
             return in_turn(e, [P, PACK + 1, C], F32, "staging")
 
         def product(stage, z, s):
             d = stage[:, 0:PACK, :]
-            nc.gpsimd.tensor_tensor(d, z[:], s[:], ALU.mult)
+            for t in range(PACK):
+                nc.gpsimd.tensor_tensor(d[:, t, :], z[:, t, :], s[:, t, :], ALU.mult)
             return d
 
         def quantize(grouped, kind, depth):
@@ -138,7 +149,7 @@ def tile_moe_bdx_mlp_silu_kernel(tc, dyT, a, w2_words, w2_scales, w1_words, w1_s
             for t in range(PACK):
                 nc.vector.tensor_tensor(g[:, t, :], dy[t][:].indirect(slots(e)), gates[e][:], ALU.mult)
             g_grouped = ring.tile([P, C, PACK], BF16, name="g_grouped", align_bytes=64)
-            nc.scalar.copy(out=g_grouped[:], in_=g[:].rearrange("p t c -> p c t"))
+            interleave(g_grouped, g)
             return quantize(g_grouped, "g", E)
 
         def multiply(e, minus_d, g_codes, g_scales):
@@ -166,7 +177,7 @@ def tile_moe_bdx_mlp_silu_kernel(tc, dyT, a, w2_words, w2_scales, w1_words, w1_s
                 for t in range(0, PACK, 2):
                     nc.gpsimd.tensor_tensor(da[:, t : t + 2, :], dh_copy[:, t : t + 2, :], minus_d[:, t : t + 2, :], ALU.mult)
             da_grouped = in_turn(max(e, 1), [P, C, PACK], BF16, "da_grouped")
-            nc.scalar.copy(out=da_grouped[:], in_=da[:].rearrange("p t c -> p c t"))
+            interleave(da_grouped, da)
             da_codes, da_scales = quantize(da_grouped, "da", 2)
             return da_codes, da_scales
 
@@ -204,9 +215,10 @@ def tile_moe_bdx_mlp_silu_kernel(tc, dyT, a, w2_words, w2_scales, w1_words, w1_s
         codes = [gather(0)]
         operand = multiply(0, derivative(0), *codes[0])
         first = project_first(0, operand)
-        d = derivative(1)
+        factors = derivative(1)
         codes += [gather(e) for e in range(1, E)]
         window = [keep.tile([P, T], F32, name=f"window{m}", tag=f"columns{m}") for m in range(K_TILES)]
+        d = product(staging(0), *factors)
         for e in range(1, E):
             following = multiply(e, d, *codes[e])
             stage = staging(e)

from contextlib import ExitStack

import concourse.mybir as mybir

K, T, E, C, H, N = 768, 2048, 4, 512, 512, 512
P = 128
PACK = 4
K_TILES = K // P

F32 = mybir.dt.float32
BF16 = mybir.dt.bfloat16
I32 = mybir.dt.int32
U32 = mybir.dt.uint32
U16 = mybir.dt.uint16
U8 = mybir.dt.uint8
FP4X4 = mybir.dt.float4_e2m1fn_x4
FP8X4 = mybir.dt.float8_e5m2_x4
ACT = mybir.ActivationFunctionType
ALU = mybir.AluOpType

FLOPS = 2 * E * C * (N * H + H * K)
BYTES = 4 * (N * T + H * E * C + E * C + K * T) + 2 * E * C + E * (N * H + H * K) * 17 // 32


def tile_moe_bdx_mlp_silu_kernel(tc, dyT, a, w2_words, w2_scales, w1_words, w1_scales, gate, offs, out):
    nc = tc.nc
    with ExitStack() as ctx:
        keep = ctx.enter_context(tc.tile_pool(name="keep", bufs=1))
        ring = ctx.enter_context(tc.tile_pool(name="ring", bufs=2))
        psum_h = ctx.enter_context(tc.psum_pool(name="psum_h", bufs=4))
        psum_x = ctx.enter_context(tc.psum_pool(name="psum_x", bufs=4))

        offsets = keep.tile([P, E * C // 16], U16, name="offsets")
        dy = [keep.tile([P, T], F32, name=f"dy{t}", tag=f"columns{t}") for t in range(PACK)]
        pre = [keep.tile([P, PACK, C], F32, name=f"pre{e}") for e in range(E)]
        w2_raw = keep.tile([P, E, 2 * H], U8, name="w2_raw", align_bytes=64)
        w2 = keep.tile([P, E, 2 * H], U8, name="w2", align_bytes=64)
        w2_sraw = keep.tile([P, E, H], U8, name="w2_sraw", align_bytes=64)
        w2_s = keep.tile([P, E, H], U8, name="w2_s", align_bytes=64)
        w1 = keep.tile([P, E, 2 * K], U8, name="w1", align_bytes=64)
        w1_s = keep.tile([P, E, K], U8, name="w1_s", align_bytes=64)

        def in_turn(i, shape, dtype, name):
            return ring.tile(shape, dtype, name=name, tag=f"turn{i % 2}", align_bytes=64, bufs=1)

        gates = [keep.tile([P, C], F32, name=f"gates{e}") for e in range(E - 1)]
        gates.append(in_turn(0, [P, C], F32, "gates_last"))

        nc.vector.memset(w2_sraw[:].bitcast(I32), 0)
        nc.vector.memset(w1_s[:].bitcast(I32), 0)
        warm = keep.tile([P, 8], F32, name="warm")
        nc.vector.memset(warm[:], 0.0)
        nc.scalar.activation(warm[:], warm[:], ACT.Sigmoid)

        dy_rows = dyT.rearrange("(p t) j -> p t j", t=PACK)
        a_rows = a.rearrange("(p t) j -> p t j", t=PACK)

        def load_scales(planes, scales):
            for q in range(4):
                nc.sync.dma_start(
                    out=planes[32 * q : 32 * q + 4].bitcast(I32),
                    in_=scales[:, 0, 4 * q : 4 * q + 4, :].rearrange("e f n -> f e n").bitcast(I32),
                )

        def load_w2(e):
            nc.sync.dma_start(
                out=w2_raw[:, e : e + 2].bitcast(I32), in_=w2_words[e : e + 2].rearrange("e o p n -> p (e o) n").bitcast(I32)
            )

        def load_gates(e):
            nc.sync.dma_start(out=gates[e][:], in_=gate[0:P, e * C : (e + 1) * C])

        def load_dy(t):
            nc.sync.dma_start(out=dy[t][:], in_=dy_rows[:, t, :])

        def load_pre(e):
            nc.sync.dma_start(out=pre[e][:], in_=a_rows[:, :, e * C : (e + 1) * C])

        nc.sync.dma_start(out=offsets[:], in_=offs)
        load_scales(w2_sraw, w2_scales)
        load_w2(0)
        for i in range(3):
            load_gates(i)
            load_dy(i)
        load_pre(0)
        load_dy(3)
        load_w2(2)
        load_gates(3)
        load_pre(1)
        load_scales(w1_s, w1_scales)
        nc.sync.dma_start(out=w1[:].bitcast(I32), in_=w1_words.rearrange("e o p n -> p (e o) n").bitcast(I32))
        load_pre(2)
        load_pre(3)

        nc.vector.tensor_copy(
            out=w2_s[:].rearrange("p e (t m) -> p e t m", t=PACK),
            in_=w2_sraw[:].rearrange("p e (m t) -> p e t m", t=PACK),
        )
        for e in (0, 2):
            nc.vector.tensor_copy(
                out=w2[:, e : e + 2].bitcast(U16).rearrange("p e (t m) -> p e t m", t=PACK),
                in_=w2_raw[:, e : e + 2].bitcast(U16).rearrange("p e (m t) -> p e t m", t=PACK),
            )

        def interleave(grouped, planes):
            nc.scalar.copy(
                out=grouped[:].rearrange("p (c i) t -> p c t i", i=4),
                in_=planes[:].rearrange("p t (c i) -> p c t i", i=4),
            )

        def slots(e):
            return offsets[:, e * C // 16 : (e + 1) * C // 16]

        def derivative(e):
            other = ring.tile([P, PACK, C], F32, name="other")
            if e % 2 == 0:
                for t in range(0, PACK, 2):
                    nc.scalar.activation(other[:, t : t + 2, :], pre[e][:, t : t + 2, :], ACT.Sigmoid)
                for t in range(0, PACK, 2):
                    nc.scalar.activation(pre[e][:, t : t + 2, :], pre[e][:, t : t + 2, :], ACT.Silu, scale=-1.0)
                z, s = pre[e], other
            else:
                nc.scalar.activation(other[:], pre[e][:], ACT.Silu, scale=-1.0)
                nc.scalar.activation(pre[e][:], pre[e][:], ACT.Sigmoid)
                z, s = other, pre[e]
            if e == 0:
                nc.vector.scalar_tensor_tensor(out=other[:], in0=z[:], scalar=1.0, in1=s[:], op0=ALU.subtract, op1=ALU.mult)
                return other[:]
            nc.scalar.activation(z[:], z[:], ACT.Identity, bias=-1.0)
            return z, s

        def staging(e):
            return in_turn(e, [P, PACK + 1, C], F32, "staging")

        def product(stage, z, s):
            d = stage[:, 0:PACK, :]
            for t in range(PACK):
                nc.gpsimd.tensor_tensor(d[:, t, :], z[:, t, :], s[:, t, :], ALU.mult)
            return d

        def quantize(grouped, kind, depth):
            codes = ring.tile([P, C], U32, name=f"codes_{kind}", align_bytes=64, bufs=depth)
            scales = ring.tile([P, C], U8, name=f"scales_{kind}", align_bytes=64, bufs=depth)
            nc.vector.quantize_mx(out=codes[:].bitcast(FP8X4), scales=scales[:], in_=grouped[:].rearrange("p c t -> p (c t)"))
            return codes, scales

        def gather(e):
            g = ring.tile([P, PACK, C], F32, name="g", bufs=3)
            for t in range(PACK):
                nc.vector.tensor_tensor(g[:, t, :], dy[t][:].indirect(slots(e)), gates[e][:], ALU.mult)
            g_grouped = ring.tile([P, C, PACK], BF16, name="g_grouped", align_bytes=64)
            interleave(g_grouped, g)
            return quantize(g_grouped, "g", E)

        def multiply(e, minus_d, g_codes, g_scales):
            da = ring.tile([P, PACK, C], BF16, name="da", align_bytes=64, bufs=1)
            if e > 0:
                dh_copy = ring.tile([P, PACK, C], F32, name="dh_copy", bufs=1)
            for t in range(PACK):
                dh = psum_h.tile([P, C], F32, name="dh")
                nc.tensor.matmul_mx(
                    out=dh[:],
                    lhsT=w2[:, e, 2 * P * t : 2 * P * (t + 1)].bitcast(FP4X4),
                    lhsT_scale=w2_s[:, e, P * t : P * (t + 1)],
                    rhs=g_codes[:].bitcast(FP8X4),
                    rhs_scale=g_scales[:],
                    start=True,
                    stop=True,
                )
                if e == 0:
                    nc.vector.scalar_tensor_tensor(
                        out=da[:, t, :], in0=dh[:], scalar=-1.0, in1=minus_d[:, t, :], op0=ALU.mult, op1=ALU.mult
                    )
                else:
                    nc.scalar.activation(dh_copy[:, t, :], dh[:], ACT.Copy, scale=-1.0)
            if e > 0:
                for t in range(0, PACK, 2):
                    nc.gpsimd.tensor_tensor(da[:, t : t + 2, :], dh_copy[:, t : t + 2, :], minus_d[:, t : t + 2, :], ALU.mult)
            da_grouped = in_turn(max(e, 1), [P, C, PACK], BF16, "da_grouped")
            interleave(da_grouped, da)
            da_codes, da_scales = quantize(da_grouped, "da", 2)
            return da_codes, da_scales

        def project(e, m, da_codes, da_scales, result):
            dx = psum_x.tile([P, C], F32, name="dx")
            nc.tensor.matmul_mx(
                out=dx[:],
                lhsT=w1[:, e, 2 * P * m : 2 * P * (m + 1)].bitcast(FP4X4),
                lhsT_scale=w1_s[:, e, P * m : P * (m + 1)],
                rhs=da_codes[:].bitcast(FP8X4),
                rhs_scale=da_scales[:],
                start=True,
                stop=True,
            )
            nc.scalar.copy(out=result, in_=dx[:])

        def project_first(e, operand):
            results = []
            for m in range(K_TILES - 1):
                result = ring.tile([P, C], F32, name="result", bufs=6)
                project(e, m, *operand, result[:])
                results.append(result[:])
            return results

        def project_last(e, operand, stage):
            project(e, K_TILES - 1, *operand, stage[:, PACK, :])
            return [stage[:, PACK, :]]

        def put_back(e, results):
            for m in range(K_TILES):
                nc.vector.tensor_copy(window[m][:].indirect(slots(e)), results[m])
                if e == E - 1:
                    nc.sync.dma_start(out=out[m * P : (m + 1) * P, :], in_=window[m][:])

        codes = [gather(0)]
        operand = multiply(0, derivative(0), *codes[0])
        first = project_first(0, operand)
        factors = derivative(1)
        codes += [gather(e) for e in range(1, E)]
        window = [keep.tile([P, T], F32, name=f"window{m}", tag=f"columns{m}") for m in range(K_TILES)]
        d = product(staging(0), *factors)
        for e in range(1, E):
            following = multiply(e, d, *codes[e])
            stage = staging(e)
            results = first + project_last(e - 1, operand, stage)
            if e + 1 < E:
                d = product(stage, *derivative(e + 1))
            put_back(e - 1, results)
            operand = following
            first = project_first(e, operand)
        stage = staging(E)
        put_back(E - 1, first + project_last(E - 1, operand, stage))
